import numpy as np
import ml_dtypes


def mxq(x, axis, fmt="e4m3"):
    dtype, down = {"e4m3": (ml_dtypes.float8_e4m3fn, 7), "e5m2": (ml_dtypes.float8_e5m2, 14)}[fmt]
    v = np.moveaxis(np.asarray(x, np.float32).astype(ml_dtypes.bfloat16).astype(np.float64), axis, -1)
    blocks = v.reshape(v.shape[:-1] + (-1, 32))
    amax = np.abs(blocks).max(-1, keepdims=True)
    byte = np.maximum(np.where(amax > 0, np.frexp(amax)[1] - 1 + 127, 0) - down, 1)
    scale = np.exp2(byte - 127.0)
    codes = (blocks / scale).astype(np.float32).astype(dtype).astype(np.float64)
    return np.moveaxis((codes * scale).reshape(v.shape), -1, axis)


WIDE = False


def mx_kscale(k):
    if not WIDE:
        return np.ones(k)
    levels = np.array([10, -10, 5, -5, 0])
    if k % 512:
        return np.exp2(np.random.permutation(np.resize(levels, k // 32))).repeat(32)
    a = np.empty((k // 512, 16))
    for p in range(k // 512):
        a[p, :8] = np.random.permutation(np.resize(levels, 8))
        for g in range(8):
            far = levels[np.abs(levels - a[p, g]) >= 10]
            a[p, g + 8] = far[np.random.randint(len(far))]
    return np.exp2(a.ravel()).repeat(32)


def f64(x):
    return np.asarray(x).astype(np.float64)


def striped(idx):
    return np.tile(np.asarray(idx).reshape(-1, 16).T, (8, 1)).astype(np.uint16)


def unstriped(offs):
    return offs[:16].T.reshape(-1).astype(np.int64)


E2M1 = np.array([0.0, 0.5, 1.0, 1.5, 2.0, 3.0, 4.0, 6.0, -0.0, -0.5, -1.0, -1.5, -2.0, -3.0, -4.0, -6.0])


def pack_weight(w, fmt):
    k, n = w.shape
    w = f64(np.asarray(w, np.float32).astype(ml_dtypes.bfloat16)).reshape(k // 32, 32, n)
    amax = np.abs(w).max(1)
    if fmt == "e4m3":
        byte = np.frexp(amax)[1] - 1 + 127 - 7
    else:
        mant, ex = np.frexp(amax / 6.0)
        byte = np.where(mant > 0.5, ex, ex - 1) + 127
    byte = np.clip(np.where(amax > 0, byte, 1), 1, 254)
    scaled = (w * np.exp2(127.0 - byte)[:, None, :]).reshape(k, n).astype(np.float32)
    by_word = np.ascontiguousarray(scaled.reshape(k // 512, 128, 4, n).transpose(0, 1, 3, 2))
    if fmt == "e4m3":
        words = by_word.astype(ml_dtypes.float8_e4m3fn).view(np.uint8)
    else:
        c = by_word.astype(ml_dtypes.float4_e2m1fn).view(np.uint8) & 0xF
        words = (c[..., 0::2] | (c[..., 1::2] << 4)).reshape(k // 512, 128, 2 * n)
    return np.ascontiguousarray(words), np.ascontiguousarray(byte.astype(np.uint8).reshape(k // 512, 16, n))


def unpack_weight(words, scales, fmt):
    g, _, n = scales.shape
    words = np.ascontiguousarray(words).reshape(g, 128, n, -1)
    if fmt == "e4m3":
        vals = words.view(ml_dtypes.float8_e4m3fn).astype(np.float64)
    else:
        nib = np.empty((g, 128, n, 4), np.uint8)
        nib[..., 0::2] = words & 0xF
        nib[..., 1::2] = words >> 4
        vals = E2M1[nib]
    vals = vals * np.repeat(np.exp2(scales.astype(np.float64) - 127.0), 8, axis=1)[..., None]
    return vals.transpose(0, 1, 3, 2).reshape(g * 512, n)


def softplus(v):
    return np.log(1.0 + np.exp(v))


D, K, R, T, I, Q, G = 512, 512, 512, 2048, 512, 128, 64


def setup_inputs():
    n = np.random.standard_normal
    idx3 = np.random.permutation(I)[:I]
    idx = np.random.permutation(T)[:I]
    fd = mx_kscale(D)
    fk = mx_kscale(K)
    fr = mx_kscale(R)
    keysp = pack_weight(n((D, T)) / fd[:, None], "e4m3")
    tabp = pack_weight(n((K, T)) / fk[:, None], "e4m3")
    return {
        "query": (n((D, Q)) * 0.6 / np.sqrt(D) * fd[:, None]).astype(np.float32),
        "keys_words": keysp[0],
        "keys_scales": keysp[1],
        "sharp": (np.random.uniform(1.0, 3.0, (Q, 1))).astype(np.float32),
        "tab_words": tabp[0],
        "tab_scales": tabp[1],
        "w1": (n((K, R)) * 1 / np.sqrt(K) * fk[:, None]).astype(np.float32),
        "lam": (np.random.uniform(0.3, 1.0, (R, 1))).astype(np.float32),
        "gout": (n((R, Q)) * 1 / np.sqrt(R) * fr[:, None]).astype(np.float32),
        "hsc": (np.random.uniform(0.7, 1.4, (R, 1)) / fr[:, None]).astype(np.float32),
        "old": (0.5 * n((Q, T))).astype(np.float32),
        "offs3": striped(idx3),
        "offs": striped(idx),
    }


def reference(query, keys_words, keys_scales, sharp, tab_words, tab_scales, w1, lam, gout, hsc, old, offs3, offs):
    idx3 = unstriped(offs3)
    idx = unstriped(offs)
    keysu = unpack_weight(keys_words, keys_scales, "e4m3")
    tabu = unpack_weight(tab_words, tab_scales, "e4m3")
    queryq = mxq(f64(query), 0, "e4m3")
    keysidxg = keysu[:, idx]
    a = queryq.T @ keysidxg
    p = np.exp(a)
    s = p.reshape(Q, G, I // G).sum(axis=2)
    ms = a.reshape(Q, G, I // G).mean(axis=2) * f64(sharp)
    pg = np.exp(ms - np.max(ms, axis=1, keepdims=True))
    z = np.sum(pg, axis=1, keepdims=True)
    sh = pg / z / s
    rr = np.repeat(sh, I // G, axis=1)
    w1q = mxq(f64(w1), 0, "e4m3")
    tabidxg = tabu[:, idx]
    zh = w1q.T @ tabidxg
    ht = softplus(zh)
    hv = ht + ht[:, idx3] * f64(lam)
    hs1 = hv * f64(hsc)
    goutq = mxq(f64(gout), 0, "e4m3")
    hs1q = mxq(hs1, 0, "e4m3")
    c0 = goutq.T @ hs1q
    drr = c0 * p
    dsh = drr.reshape(Q, G, I // G).sum(axis=2)
    dz = np.sum(dsh / s * pg / np.square(z) * (-1.0), axis=1, keepdims=True)
    dpg = dsh / s / z + dz
    dms = dpg * pg
    e1 = dms * f64(sharp) / 8.0
    r1 = np.repeat(e1, I // G, axis=1)
    ds = dsh * pg / z / np.square(s) * (-1.0)
    r2 = np.repeat(ds, I // G, axis=1)
    dp = c0 * rr + r2
    da = r1 + dp * p
    gs = da * 512.0
    gf = np.zeros((Q, T))
    gf[:, idx] = gs
    y = f64(old) + gf
    return y

@@ -1,0 +1,285 @@
+from contextlib import ExitStack
+
+import concourse.mybir as mybir
+
+FLOPS = 402653184
+
+F32 = mybir.dt.float32
+BF16 = mybir.dt.bfloat16
+I32 = mybir.dt.int32
+U32 = mybir.dt.uint32
+U16 = mybir.dt.uint16
+U8 = mybir.dt.uint8
+FP8X4 = mybir.dt.float8_e4m3fn_x4
+ALU = mybir.AluOpType
+ACT = mybir.ActivationFunctionType
+AX = mybir.AxisListType
+
+P = 128
+PACK = 4
+T = 2048
+SLOTS = 512
+GROUPS = 64
+GSIZE = 8
+HALF = 256
+LINEAR_FROM = 30.0
+STORE_WIDTHS = (640, 640, 512, 256)
+
+
+def tile_attend_blrlent_bygroup_kernel(
+    tc, query, keys_words, keys_scales, sharp, tab_words, tab_scales, w1, lam, gout, hsc, old, offs3, offs, out
+):
+    nc = tc.nc
+    with ExitStack() as ctx:
+        sb = ctx.enter_context(tc.tile_pool(name="sb", bufs=1))
+        ps = ctx.enter_context(tc.psum_pool(name="ps", bufs=1))
+
+        def tile(name, shape, dtype, tag=None):
+            return sb.tile(shape, dtype, name=name, tag=tag or name, align_bytes=64)
+
+        def by_group(ap):
+            return ap.rearrange("p (g j) -> p g j", j=GSIZE)
+
+        def spread(ap, groups):
+            return ap.unsqueeze(2).to_broadcast([P, groups, GSIZE])
+
+        def load_scales(dst, src, queue):
+            for quad in range(4):
+                queue.dma_start(
+                    out=dst[32 * quad : 32 * quad + 4, :].bitcast(I32),
+                    in_=src[0, 4 * quad : 4 * quad + 4, :].bitcast(I32),
+                )
+
+        def load_words(dst, src):
+            nc.sync.dma_start(out=dst[:], in_=src[0].rearrange("p n r -> p (n r)").bitcast(I32))
+
+        def interleave(engine_copy, dst, src):
+            engine_copy(
+                out=dst.rearrange("p (c i t) -> p c t i", i=4, t=PACK),
+                in_=src.rearrange("p t (c i) -> p c t i", i=4),
+            )
+
+        tab_s = tile("tab_s", [P, T], U8)
+        key_s = tile("key_s", [P, T], U8)
+        gf = tile("gf", [P, T], F32)
+        nc.vector.memset(tab_s[:].bitcast(I32), 0)
+        nc.gpsimd.memset(key_s[:].bitcast(I32), 0)
+        nc.vector.memset(gf[:], 0.0)
+
+        idx = tile("idx", [P, SLOTS // 16], U16)
+        idx3 = tile("idx3", [P, SLOTS // 16], U16)
+        tab_w = tile("tab_w", [P, T], I32)
+        key_w = tile("key_w", [P, T], I32)
+        w_raw = [tile("w_raw%d" % h, [P, PACK, HALF], F32) for h in range(2)]
+        q_raw = tile("q_raw", [P, PACK, P], F32)
+        go_raw = tile("go_raw", [P, PACK, P], F32)
+        old_sb = tile("old_sb", [P, T], F32)
+        sharp_sb = tile("sharp_sb", [P, 1], F32)
+        lam_sb = tile("lam_sb", [P, PACK], F32)
+        hsc_sb = tile("hsc_sb", [P, PACK], F32)
+
+        w_rows = w1.rearrange("(p j) c -> p j c", j=PACK)
+        tab_stage = tile("tab_stage", [P, T], U8)
+        load_scales(tab_stage, tab_scales, nc.sync)
+        nc.sync.dma_start(idx[:], offs)
+        nc.sync.dma_start(out=w_raw[0][:], in_=w_rows[:, :, :HALF])
+        load_words(tab_w, tab_words)
+        nc.sync.dma_start(out=w_raw[1][:], in_=w_rows[:, :, HALF:])
+        load_scales(key_s, keys_scales, nc.gpsimd)
+        nc.sync.dma_start(out=q_raw[:], in_=query.rearrange("(p j) c -> p j c", j=PACK))
+        load_words(key_w, keys_words)
+        nc.sync.dma_start(out=sharp_sb[:], in_=sharp)
+        nc.sync.dma_start(out=lam_sb[:], in_=lam.rearrange("(p j) o -> p (j o)", j=PACK))
+        nc.sync.dma_start(out=hsc_sb[:], in_=hsc.rearrange("(p j) o -> p (j o)", j=PACK))
+        nc.sync.dma_start(idx3[:], offs3)
+        nc.sync.dma_start(out=go_raw[:], in_=gout.rearrange("(p j) c -> p j c", j=PACK))
+        nc.sync.dma_start(out=old_sb[:], in_=old)
+
+        tab_sg = tile("tab_sg", [P, SLOTS], U8)
+        tab_wg = tile("tab_wg", [P, SLOTS], U32)
+        for quad in range(4):
+            rows = slice(32 * quad, 32 * quad + 4)
+            nc.vector.tensor_copy(tab_s[rows, :].bitcast(I32), tab_stage[rows, :].bitcast(I32))
+        nc.vector.tensor_copy(tab_sg[:], tab_s[:].indirect(idx[:]))
+        nc.vector.tensor_copy(tab_wg[:], tab_w[:].bitcast(U32).indirect(idx[:]))
+
+        w_bf = tile("w_bf", [P, PACK, P, PACK], BF16)
+        for h, cast in enumerate((nc.scalar.copy, nc.vector.tensor_copy)):
+            cast(
+                out=w_bf[:, :, h * 64 : (h + 1) * 64, :].rearrange("p t m j -> p m j t"),
+                in_=w_raw[h][:].rearrange("p j (m t) -> p m j t", t=PACK),
+            )
+        w_c = tile("w_c", [P, PACK * P], U32)
+        w_s = tile("w_s", [P, PACK * P], U8)
+        zh = [ps.tile([P, SLOTS], F32, name="zh%d" % t) for t in range(PACK)]
+        ex = [tile("ex%d" % t, [P, SLOTS], F32) for t in range(PACK)]
+        for t in range(PACK):
+            cols = slice(t * P, (t + 1) * P)
+            nc.vector.quantize_mx(
+                out=w_c[:, cols].bitcast(FP8X4), scales=w_s[:, cols], in_=w_bf[:, t].rearrange("p m j -> p (m j)")
+            )
+            nc.tensor.matmul_mx(
+                out=zh[t][:], lhsT=w_c[:, cols].bitcast(FP8X4), lhsT_scale=w_s[:, cols],
+                rhs=tab_wg[:].bitcast(FP8X4), rhs_scale=tab_sg[:], start=True, stop=True,
+            )
+            nc.scalar.activation(ex[t][:], zh[t][:], ACT.Exp)
+
+        key_sg = tile("key_sg", [P, SLOTS], U8, tag="w_bf")
+        key_wg = tile("key_wg", [P, SLOTS], U32)
+        q_bf = tile("q_bf", [P, P * PACK], BF16)
+        q_c = tile("q_c", [P, P], U32)
+        q_s = tile("q_s", [P, P], U8)
+        nc.vector.tensor_copy(key_sg[:], key_s[:].indirect(idx[:]))
+        interleave(nc.vector.tensor_copy, q_bf[:], q_raw[:])
+        nc.vector.tensor_copy(key_wg[:], key_w[:].bitcast(U32).indirect(idx[:]))
+        nc.vector.quantize_mx(out=q_c[:].bitcast(FP8X4), scales=q_s[:], in_=q_bf[:])
+        a_ps = ps.tile([P, SLOTS], F32, name="a_ps")
+        nc.tensor.matmul_mx(
+            out=a_ps[:], lhsT=q_c[:].bitcast(FP8X4), lhsT_scale=q_s[:],
+            rhs=key_wg[:].bitcast(FP8X4), rhs_scale=key_sg[:], start=True, stop=True,
+        )
+        sh8 = tile("sh8", [P, 1], F32)
+        nsh8 = tile("nsh8", [P, 1], F32)
+        lh = tile("lh", [P, PACK], F32)
+        nc.vector.tensor_scalar(sh8[:], sharp_sb[:], 1.0 / GSIZE, None, ALU.mult)
+        nc.vector.tensor_scalar(nsh8[:], sharp_sb[:], -1.0 / GSIZE, None, ALU.mult)
+        nc.vector.tensor_tensor(lh[:], lam_sb[:], hsc_sb[:], ALU.mult)
+        a_max = tile("a_max", [P, GROUPS], F32)
+        a_sum = tile("a_sum", [P, GROUPS], F32)
+        a_rel = tile("a_rel", [P, SLOTS], F32)
+        nms = tile("nms", [P, GROUPS], F32)
+        nms_min = tile("nms_min", [P, 1], F32)
+        nc.vector.tensor_reduce(a_max[:], by_group(a_ps[:]), AX.X, ALU.max)
+        nc.vector.tensor_reduce(a_sum[:], by_group(a_ps[:]), AX.X, ALU.add)
+        nc.vector.tensor_tensor(by_group(a_rel[:]), by_group(a_ps[:]), spread(a_max[:], GROUPS), ALU.subtract)
+        nc.vector.tensor_scalar(nms[:], a_sum[:], nsh8[:], None, ALU.mult, ALU.min, accum_out=nms_min[:])
+
+        go_bf = tile("go_bf", [P, P * PACK], BF16)
+        go_c = tile("go_c", [P, P], U32)
+        go_s = tile("go_s", [P, P], U8)
+
+        ln = [tile("ln%d" % t, [P, SLOTS], F32) for t in range(PACK)]
+        ht = [tile("ht%d" % t, [P, SLOTS], F32) for t in range(PACK)]
+        own = [tile("own%d" % t, [P, SLOTS], F32) for t in range(PACK)]
+        link = [[tile("link%d_%d" % (t, h), [P, HALF], F32) for h in range(2)] for t in range(PACK)]
+        hs = [tile("hs%d" % h, [P, PACK, HALF], BF16) for h in range(2)]
+        for t in range(PACK):
+            nc.scalar.activation(ln[t][:], ex[t][:], ACT.Ln, bias=1.0)
+
+        def softplus(t):
+            nc.vector.scalar_tensor_tensor(ht[t][:], ln[t][:], LINEAR_FROM, zh[t][:], ALU.min, ALU.max)
+            nc.scalar.activation(own[t][:], ht[t][:], ACT.Copy, scale=hsc_sb[:, t : t + 1])
+
+        def look_up(t, h):
+            nc.vector.tensor_copy(link[t][h][:], ht[t][:].indirect(idx3[:, 16 * h : 16 * (h + 1)]))
+
+        def combine(t, h):
+            nc.vector.scalar_tensor_tensor(
+                hs[h][:, t, :], link[t][h][:], lh[:, t : t + 1], own[t][:, h * HALF : (h + 1) * HALF], ALU.mult, ALU.add
+            )
+
+        softplus(0)
+        softplus(1)
+        for t in range(PACK):
+            look_up(t, 0)
+            if t + 2 < PACK:
+                softplus(t + 2)
+            if t > 0:
+                combine(t - 1, 0)
+        look_up(0, 1)
+        combine(PACK - 1, 0)
+
+        p_rel = tile("p_rel", [P, SLOTS], F32)
+        pg = tile("pg", [P, GROUPS], F32)
+        z = tile("z", [P, 1], F32)
+        nc.scalar.activation(p_rel[:], a_rel[:], ACT.Exp)
+        nc.scalar.activation(pg[:], nms[:], ACT.Exp, bias=nms_min[:], scale=-1.0, accum_out=z[:])
+        interleave(nc.scalar.copy, go_bf[:], go_raw[:])
+
+        hs_bf = [tile("hs_bf%d" % h, [P, HALF * PACK], BF16) for h in range(2)]
+        hs_c = [tile("hs_c%d" % h, [P, HALF], U32) for h in range(2)]
+        hs_s = [tile("hs_s%d" % h, [P, HALF], U8) for h in range(2)]
+        c0 = [ps.tile([P, HALF], F32, name="c0_%d" % h) for h in range(2)]
+        interleave(nc.scalar.copy, hs_bf[0][:], hs[0][:])
+
+        s = tile("s", [P, GROUPS], F32)
+        rs = tile("rs", [P, GROUPS], F32)
+        rz = tile("rz", [P, 1], F32)
+        wgt = tile("wgt", [P, SLOTS], F32)
+        rest = tile("rest", [P, SLOTS], F32)
+        k_out = tile("k_out", [P, 1], F32)
+        k_mean = tile("k_mean", [P, 1], F32)
+        share = tile("share", [P, SLOTS], F32)
+
+        nc.vector.tensor_reduce(s[:], by_group(p_rel[:]), AX.X, ALU.add)
+        look_up(1, 1)
+        nc.vector.reciprocal(rs[:], s[:])
+        nc.vector.reciprocal(rz[:], z[:])
+        combine(0, 1)
+        nc.vector.tensor_tensor(by_group(wgt[:]), by_group(p_rel[:]), spread(rs[:], GROUPS), ALU.mult)
+        nc.scalar.activation(rest[:], wgt[:], ACT.Identity, bias=sh8[:], scale=-1.0)
+        nc.scalar.activation(k_out[:], rz[:], ACT.Copy, scale=512.0)
+        nc.scalar.activation(k_mean[:], rz[:], ACT.Copy, scale=nsh8[:])
+        nc.scalar.activation(by_group(share[:]), spread(pg[:], GROUPS), ACT.Copy, scale=k_out[:])
+        nc.vector.quantize_mx(out=go_c[:].bitcast(FP8X4), scales=go_s[:], in_=go_bf[:])
+        look_up(2, 1)
+        combine(1, 1)
+
+        def product(h):
+            nc.vector.quantize_mx(out=hs_c[h][:].bitcast(FP8X4), scales=hs_s[h][:], in_=hs_bf[h][:])
+            nc.tensor.matmul_mx(
+                out=c0[h][:], lhsT=go_c[:].bitcast(FP8X4), lhsT_scale=go_s[:],
+                rhs=hs_c[h][:].bitcast(FP8X4), rhs_scale=hs_s[h][:], start=True, stop=True,
+            )
+
+        cw = tile("cw", [P, SLOTS], F32)
+        mean = tile("mean", [P, GROUPS], F32)
+        term = tile("term", [P, SLOTS], F32)
+        inner = tile("inner", [P, SLOTS], F32)
+        junk = tile("junk", [P, GROUPS], F32)
+        shift = tile("shift", [P, 1], F32)
+
+        def cols_of(h):
+            return slice(h * HALF, (h + 1) * HALF)
+
+        def groups_of(h):
+            return slice(h * GROUPS // 2, (h + 1) * GROUPS // 2)
+
+        def weigh(h):
+            nc.vector.tensor_tensor(cw[:, cols_of(h)], c0[h][:], wgt[:, cols_of(h)], ALU.mult)
+
+        def group_mean(h):
+            nc.vector.tensor_reduce(mean[:, groups_of(h)], by_group(cw[:, cols_of(h)]), AX.X, ALU.add)
+
+        def mean_term(h):
+            nc.vector.tensor_tensor(
+                by_group(term[:, cols_of(h)]), by_group(rest[:, cols_of(h)]),
+                spread(mean[:, groups_of(h)], GROUPS // 2), ALU.mult,
+            )
+
+        product(0)
+        look_up(3, 1)
+        combine(2, 1)
+        combine(3, 1)
+        interleave(nc.scalar.copy, hs_bf[1][:], hs[1][:])
+        weigh(0)
+        group_mean(0)
+        mean_term(0)
+        product(1)
+        weigh(1)
+        group_mean(1)
+        nc.vector.scalar_tensor_tensor(junk[:], mean[:], k_mean[:], pg[:], ALU.mult, ALU.mult, accum_out=shift[:])
+        mean_term(1)
+        for h in range(2):
+            nc.vector.scalar_tensor_tensor(
+                inner[:, cols_of(h)], term[:, cols_of(h)], shift[:], cw[:, cols_of(h)], ALU.add, ALU.add
+            )
+        nc.vector.tensor_tensor(gf[:].indirect(idx[:]), inner[:], share[:], ALU.mult)
+
+        res = tile("res", [P, T], F32)
+        start = 0
+        for width in STORE_WIDTHS:
+            cols = slice(start, start + width)
+            nc.vector.tensor_tensor(res[:, cols], gf[:, cols], old_sb[:, cols], ALU.add)
+            nc.sync.dma_start(out=out[:, cols], in_=res[:, cols])
+            start += width

@@ -23,7 +23,9 @@ GROUPS = 64
 GSIZE = 8
 HALF = 256
 LINEAR_FROM = 30.0
-STORE_WIDTHS = (640, 640, 512, 256)
+W_SPLIT = 22
+LAM_FLOOR = 2.0**-60
+STORE_WIDTHS = (256, 512, 512, 512, 256)
 
 
 def tile_attend_blrlent_bygroup_kernel(
@@ -69,46 +71,49 @@ def tile_attend_blrlent_bygroup_kernel(
         idx = tile("idx", [P, SLOTS // 16], U16)
         idx3 = tile("idx3", [P, SLOTS // 16], U16)
         tab_w = tile("tab_w", [P, T], I32)
-        key_w = tile("key_w", [P, T], I32)
+        tab_stage = tile("tab_stage", [P, T], U8)
+        key_w = tile("key_w", [P, T], I32, tag="tab_stage")
         w_raw = [tile("w_raw%d" % h, [P, PACK, HALF], F32) for h in range(2)]
         q_raw = tile("q_raw", [P, PACK, P], F32)
-        go_raw = tile("go_raw", [P, PACK, P], F32)
-        old_sb = tile("old_sb", [P, T], F32)
-        sharp_sb = tile("sharp_sb", [P, 1], F32)
-        lam_sb = tile("lam_sb", [P, PACK], F32)
-        hsc_sb = tile("hsc_sb", [P, PACK], F32)
+        go_raw = tile("go_raw", [P, PACK, P], F32, tag="w_raw1")
+        old_sb = tile("old_sb", [P, T], F32, tag="key_s")
+        sharp_sb = tile("sharp_sb", [P, 1], F32, tag="w_raw0")
+        lam_sb = tile("lam_sb", [P, PACK], F32, tag="tab_s")
+        hsc_sb = tile("hsc_sb", [P, PACK], F32, tag="tab_w")
 
-        w_rows = w1.rearrange("(p j) c -> p j c", j=PACK)
-        tab_stage = tile("tab_stage", [P, T], U8)
         load_scales(tab_stage, tab_scales, nc.sync)
         nc.sync.dma_start(idx[:], offs)
-        nc.sync.dma_start(out=w_raw[0][:], in_=w_rows[:, :, :HALF])
-        load_words(tab_w, tab_words)
-        nc.sync.dma_start(out=w_raw[1][:], in_=w_rows[:, :, HALF:])
-        load_scales(key_s, keys_scales, nc.gpsimd)
         nc.sync.dma_start(out=q_raw[:], in_=query.rearrange("(p j) c -> p j c", j=PACK))
-        load_words(key_w, keys_words)
-        nc.sync.dma_start(out=sharp_sb[:], in_=sharp)
-        nc.sync.dma_start(out=lam_sb[:], in_=lam.rearrange("(p j) o -> p (j o)", j=PACK))
-        nc.sync.dma_start(out=hsc_sb[:], in_=hsc.rearrange("(p j) o -> p (j o)", j=PACK))
+        load_words(tab_w, tab_words)
+        w_rows = w1.rearrange("(p j) c -> p j c", j=PACK)
+        for h in range(2):
+            nc.sync.dma_start(out=w_raw[h][:], in_=w_rows[:, :, h * HALF : (h + 1) * HALF])
+        load_scales(key_s, keys_scales, nc.sync)
         nc.sync.dma_start(idx3[:], offs3)
-        nc.sync.dma_start(out=go_raw[:], in_=gout.rearrange("(p j) c -> p j c", j=PACK))
-        nc.sync.dma_start(out=old_sb[:], in_=old)
 
         tab_sg = tile("tab_sg", [P, SLOTS], U8)
         tab_wg = tile("tab_wg", [P, SLOTS], U32)
         for quad in range(4):
             rows = slice(32 * quad, 32 * quad + 4)
             nc.vector.tensor_copy(tab_s[rows, :].bitcast(I32), tab_stage[rows, :].bitcast(I32))
+        load_words(key_w, keys_words)
         nc.vector.tensor_copy(tab_sg[:], tab_s[:].indirect(idx[:]))
         nc.vector.tensor_copy(tab_wg[:], tab_w[:].bitcast(U32).indirect(idx[:]))
 
         w_bf = tile("w_bf", [P, PACK, P, PACK], BF16)
-        for h, cast in enumerate((nc.scalar.copy, nc.vector.tensor_copy)):
+        q_bf = tile("q_bf", [P, P * PACK], BF16)
+        interleave(nc.scalar.copy, q_bf[:], q_raw[:])
+        for cast, h, lo, hi in (
+            (nc.scalar.copy, 0, 0, 64), (nc.scalar.copy, 1, 0, W_SPLIT), (nc.vector.tensor_copy, 1, W_SPLIT, 64)
+        ):
             cast(
-                out=w_bf[:, :, h * 64 : (h + 1) * 64, :].rearrange("p t m j -> p m j t"),
-                in_=w_raw[h][:].rearrange("p j (m t) -> p m j t", t=PACK),
+                out=w_bf[:, :, h * 64 + lo : h * 64 + hi, :].rearrange("p t m j -> p m j t"),
+                in_=w_raw[h][:, :, PACK * lo : PACK * hi].rearrange("p j (m t) -> p m j t", t=PACK),
             )
+        nc.sync.dma_start(out=lam_sb[:], in_=lam.rearrange("(p j) o -> p (j o)", j=PACK))
+        nc.sync.dma_start(out=hsc_sb[:], in_=hsc.rearrange("(p j) o -> p (j o)", j=PACK))
+        nc.sync.dma_start(out=sharp_sb[:], in_=sharp)
+        nc.sync.dma_start(out=go_raw[:], in_=gout.rearrange("(p j) c -> p j c", j=PACK))
         w_c = tile("w_c", [P, PACK * P], U32)
         w_s = tile("w_s", [P, PACK * P], U8)
         zh = [ps.tile([P, SLOTS], F32, name="zh%d" % t) for t in range(PACK)]
@@ -124,15 +129,14 @@ def tile_attend_blrlent_bygroup_kernel(
             )
             nc.scalar.activation(ex[t][:], zh[t][:], ACT.Exp)
 
-        key_sg = tile("key_sg", [P, SLOTS], U8, tag="w_bf")
         key_wg = tile("key_wg", [P, SLOTS], U32)
-        q_bf = tile("q_bf", [P, P * PACK], BF16)
+        key_sg = tile("key_sg", [P, SLOTS], U8, tag="w_bf")
+        nc.vector.tensor_copy(key_sg[:], key_s[:].indirect(idx[:]))
+        nc.sync.dma_start(out=old_sb[:], in_=old)
         q_c = tile("q_c", [P, P], U32)
         q_s = tile("q_s", [P, P], U8)
-        nc.vector.tensor_copy(key_sg[:], key_s[:].indirect(idx[:]))
-        interleave(nc.vector.tensor_copy, q_bf[:], q_raw[:])
-        nc.vector.tensor_copy(key_wg[:], key_w[:].bitcast(U32).indirect(idx[:]))
         nc.vector.quantize_mx(out=q_c[:].bitcast(FP8X4), scales=q_s[:], in_=q_bf[:])
+        nc.vector.tensor_copy(key_wg[:], key_w[:].bitcast(U32).indirect(idx[:]))
         a_ps = ps.tile([P, SLOTS], F32, name="a_ps")
         nc.tensor.matmul_mx(
             out=a_ps[:], lhsT=q_c[:].bitcast(FP8X4), lhsT_scale=q_s[:],
@@ -141,68 +145,70 @@ def tile_attend_blrlent_bygroup_kernel(
         sh8 = tile("sh8", [P, 1], F32)
         nsh8 = tile("nsh8", [P, 1], F32)
         lh = tile("lh", [P, PACK], F32)
-        nc.vector.tensor_scalar(sh8[:], sharp_sb[:], 1.0 / GSIZE, None, ALU.mult)
-        nc.vector.tensor_scalar(nsh8[:], sharp_sb[:], -1.0 / GSIZE, None, ALU.mult)
-        nc.vector.tensor_tensor(lh[:], lam_sb[:], hsc_sb[:], ALU.mult)
-        a_max = tile("a_max", [P, GROUPS], F32)
+        lam_bump = tile("lam_bump", [P, PACK], F32)
+        lam_safe = tile("lam_safe", [P, PACK], F32)
+        lam_inv = [tile("lam_inv%d" % k, [P, w], F32) for k, w in enumerate((1, 1, 2))]
+        nc.vector.tensor_tensor(lam_bump[:], lam_sb[:], lam_sb[:], ALU.mult)
+        a_max_tile = tile("a_max", [P, GROUPS], F32)
+        a_max = a_max_tile[:]
         a_sum = tile("a_sum", [P, GROUPS], F32)
-        a_rel = tile("a_rel", [P, SLOTS], F32)
+        a_rel_tile = tile("a_rel", [P, SLOTS], F32)
+        a_rel = a_rel_tile[:]
         nms = tile("nms", [P, GROUPS], F32)
         nms_min = tile("nms_min", [P, 1], F32)
-        nc.vector.tensor_reduce(a_max[:], by_group(a_ps[:]), AX.X, ALU.max)
+        nc.vector.tensor_scalar(lam_bump[:], lam_bump[:], LAM_FLOOR**2, 2.0 * LAM_FLOOR, ALU.is_lt, ALU.mult)
+        nc.vector.tensor_reduce(a_max, by_group(a_ps[:]), AX.X, ALU.max)
+        nc.vector.tensor_tensor(lam_safe[:], lam_sb[:], lam_bump[:], ALU.add)
+        nc.vector.tensor_tensor(by_group(a_rel), by_group(a_ps[:]), spread(a_max, GROUPS), ALU.subtract)
         nc.vector.tensor_reduce(a_sum[:], by_group(a_ps[:]), AX.X, ALU.add)
-        nc.vector.tensor_tensor(by_group(a_rel[:]), by_group(a_ps[:]), spread(a_max[:], GROUPS), ALU.subtract)
-        nc.vector.tensor_scalar(nms[:], a_sum[:], nsh8[:], None, ALU.mult, ALU.min, accum_out=nms_min[:])
 
-        go_bf = tile("go_bf", [P, P * PACK], BF16)
-        go_c = tile("go_c", [P, P], U32)
         go_s = tile("go_s", [P, P], U8)
 
-        ln = [tile("ln%d" % t, [P, SLOTS], F32) for t in range(PACK)]
-        ht = [tile("ht%d" % t, [P, SLOTS], F32) for t in range(PACK)]
+        ln_tags = ("ln0", "ln1", "lam_inv0", "lam_inv1")
+        ln = [tile("ln%d" % t, [P, SLOTS], F32, tag=ln_tags[t]) for t in range(PACK)]
+        ht = [tile("ht%d" % t, [P, SLOTS], F32, tag=(("a_max",) + ln_tags)[t]) for t in range(PACK)]
         own = [tile("own%d" % t, [P, SLOTS], F32) for t in range(PACK)]
         link = [[tile("link%d_%d" % (t, h), [P, HALF], F32) for h in range(2)] for t in range(PACK)]
         hs = [tile("hs%d" % h, [P, PACK, HALF], BF16) for h in range(2)]
-        for t in range(PACK):
+        nc.vector.reciprocal(lam_inv[0][:], lam_safe[:, 0:1])
+        nc.vector.reciprocal(lam_inv[1][:], lam_safe[:, 1:2])
+        nc.vector.reciprocal(lam_inv[2][:], lam_safe[:, 2:4])
+        nc.vector.tensor_tensor(lh[:], lam_safe[:], hsc_sb[:], ALU.mult)
+        nc.vector.tensor_scalar(sh8[:], sharp_sb[:], 1.0 / GSIZE, None, ALU.mult)
+        nc.vector.tensor_scalar(nsh8[:], sharp_sb[:], -1.0 / GSIZE, None, ALU.mult)
+        nc.vector.tensor_scalar(nms[:], a_sum[:], nsh8[:], None, ALU.mult, ALU.min, accum_out=nms_min[:])
+        inv_cols = (lam_inv[0][:], lam_inv[1][:], lam_inv[2][:, 0:1], lam_inv[2][:, 1:2])
+
+        def log1p(t):
             nc.scalar.activation(ln[t][:], ex[t][:], ACT.Ln, bias=1.0)
 
         def softplus(t):
             nc.vector.scalar_tensor_tensor(ht[t][:], ln[t][:], LINEAR_FROM, zh[t][:], ALU.min, ALU.max)
-            nc.scalar.activation(own[t][:], ht[t][:], ACT.Copy, scale=hsc_sb[:, t : t + 1])
+
+        def own_share(t):
+            nc.scalar.activation(own[t][:], ht[t][:], ACT.Copy, scale=inv_cols[t])
 
         def look_up(t, h):
-            nc.vector.tensor_copy(link[t][h][:], ht[t][:].indirect(idx3[:, 16 * h : 16 * (h + 1)]))
-
-        def combine(t, h):
-            nc.vector.scalar_tensor_tensor(
-                hs[h][:, t, :], link[t][h][:], lh[:, t : t + 1], own[t][:, h * HALF : (h + 1) * HALF], ALU.mult, ALU.add
+            nc.vector.tensor_tensor(
+                link[t][h][:], ht[t][:].indirect(idx3[:, 16 * h : 16 * (h + 1)]),
+                own[t][:, h * HALF : (h + 1) * HALF], ALU.add,
             )
 
-        softplus(0)
-        softplus(1)
-        for t in range(PACK):
-            look_up(t, 0)
-            if t + 2 < PACK:
-                softplus(t + 2)
-            if t > 0:
-                combine(t - 1, 0)
-        look_up(0, 1)
-        combine(PACK - 1, 0)
+        def combine(t, h):
+            if h == 0:
+                nc.scalar.activation(hs[h][:, t, :], link[t][h][:], ACT.Copy, scale=lh[:, t : t + 1])
+            else:
+                nc.vector.tensor_scalar(hs[h][:, t, :], link[t][h][:], lh[:, t : t + 1], None, ALU.mult)
 
-        p_rel = tile("p_rel", [P, SLOTS], F32)
-        pg = tile("pg", [P, GROUPS], F32)
+        late_exp = tile("late_exp", [P, SLOTS + GROUPS], F32, tag="ex%d" % (PACK - 1))
+        p_rel = late_exp[:, :SLOTS]
+        pg = late_exp[:, SLOTS:]
+        s = tile("s", [P, GROUPS], F32, tag="link2_1")
         z = tile("z", [P, 1], F32)
-        nc.scalar.activation(p_rel[:], a_rel[:], ACT.Exp)
-        nc.scalar.activation(pg[:], nms[:], ACT.Exp, bias=nms_min[:], scale=-1.0, accum_out=z[:])
-        interleave(nc.scalar.copy, go_bf[:], go_raw[:])
 
         hs_bf = [tile("hs_bf%d" % h, [P, HALF * PACK], BF16) for h in range(2)]
-        hs_c = [tile("hs_c%d" % h, [P, HALF], U32) for h in range(2)]
         hs_s = [tile("hs_s%d" % h, [P, HALF], U8) for h in range(2)]
         c0 = [ps.tile([P, HALF], F32, name="c0_%d" % h) for h in range(2)]
-        interleave(nc.scalar.copy, hs_bf[0][:], hs[0][:])
-
-        s = tile("s", [P, GROUPS], F32)
         rs = tile("rs", [P, GROUPS], F32)
         rz = tile("rz", [P, 1], F32)
         wgt = tile("wgt", [P, SLOTS], F32)
@@ -210,34 +216,20 @@ def tile_attend_blrlent_bygroup_kernel(
         k_out = tile("k_out", [P, 1], F32)
         k_mean = tile("k_mean", [P, 1], F32)
         share = tile("share", [P, SLOTS], F32)
-
-        nc.vector.tensor_reduce(s[:], by_group(p_rel[:]), AX.X, ALU.add)
-        look_up(1, 1)
-        nc.vector.reciprocal(rs[:], s[:])
-        nc.vector.reciprocal(rz[:], z[:])
-        combine(0, 1)
-        nc.vector.tensor_tensor(by_group(wgt[:]), by_group(p_rel[:]), spread(rs[:], GROUPS), ALU.mult)
-        nc.scalar.activation(rest[:], wgt[:], ACT.Identity, bias=sh8[:], scale=-1.0)
-        nc.scalar.activation(k_out[:], rz[:], ACT.Copy, scale=512.0)
-        nc.scalar.activation(k_mean[:], rz[:], ACT.Copy, scale=nsh8[:])
-        nc.scalar.activation(by_group(share[:]), spread(pg[:], GROUPS), ACT.Copy, scale=k_out[:])
-        nc.vector.quantize_mx(out=go_c[:].bitcast(FP8X4), scales=go_s[:], in_=go_bf[:])
-        look_up(2, 1)
-        combine(1, 1)
-
-        def product(h):
-            nc.vector.quantize_mx(out=hs_c[h][:].bitcast(FP8X4), scales=hs_s[h][:], in_=hs_bf[h][:])
-            nc.tensor.matmul_mx(
-                out=c0[h][:], lhsT=go_c[:].bitcast(FP8X4), lhsT_scale=go_s[:],
-                rhs=hs_c[h][:].bitcast(FP8X4), rhs_scale=hs_s[h][:], start=True, stop=True,
-            )
-
         cw = tile("cw", [P, SLOTS], F32)
         mean = tile("mean", [P, GROUPS], F32)
         term = tile("term", [P, SLOTS], F32)
         inner = tile("inner", [P, SLOTS], F32)
         junk = tile("junk", [P, GROUPS], F32)
         shift = tile("shift", [P, 1], F32)
+
+        def product(h):
+            codes = tile("hs_c%d" % h, [P, HALF], U32, tag=("link2_1", "rs")[h])
+            nc.vector.quantize_mx(out=codes[:].bitcast(FP8X4), scales=hs_s[h][:], in_=hs_bf[h][:])
+            nc.tensor.matmul_mx(
+                out=c0[h][:], lhsT=go_c[:].bitcast(FP8X4), lhsT_scale=go_s[:],
+                rhs=codes[:].bitcast(FP8X4), rhs_scale=hs_s[h][:], start=True, stop=True,
+            )
 
         def cols_of(h):
             return slice(h * HALF, (h + 1) * HALF)
@@ -257,24 +249,69 @@ def tile_attend_blrlent_bygroup_kernel(
                 spread(mean[:, groups_of(h)], GROUPS // 2), ALU.mult,
             )
 
-        product(0)
-        look_up(3, 1)
-        combine(2, 1)
-        combine(3, 1)
-        interleave(nc.scalar.copy, hs_bf[1][:], hs[1][:])
-        weigh(0)
-        group_mean(0)
-        mean_term(0)
-        product(1)
-        weigh(1)
-        group_mean(1)
-        nc.vector.scalar_tensor_tensor(junk[:], mean[:], k_mean[:], pg[:], ALU.mult, ALU.mult, accum_out=shift[:])
-        mean_term(1)
-        for h in range(2):
+        def scatter(h):
+            nc.vector.tensor_tensor(
+                gf[:].indirect(idx[:, 16 * h : 16 * (h + 1)]), inner[:, cols_of(h)], share[:, cols_of(h)], ALU.mult
+            )
+
+        def add_up(h):
             nc.vector.scalar_tensor_tensor(
                 inner[:, cols_of(h)], term[:, cols_of(h)], shift[:], cw[:, cols_of(h)], ALU.add, ALU.add
             )
-        nc.vector.tensor_tensor(gf[:].indirect(idx[:]), inner[:], share[:], ALU.mult)
+
+        log1p(0)
+        log1p(1)
+        softplus(0)
+        own_share(0)
+        log1p(2)
+        softplus(1)
+        own_share(1)
+        log1p(3)
+        look_up(0, 0)
+        softplus(2)
+        own_share(2)
+        look_up(1, 0)
+        softplus(3)
+        own_share(3)
+        nc.scalar.activation(p_rel, a_rel, ACT.Exp)
+        nc.scalar.activation(pg, nms[:], ACT.Exp, bias=nms_min[:], scale=-1.0, accum_out=z[:])
+        look_up(0, 1)
+        look_up(1, 1)
+        look_up(2, 0)
+        look_up(3, 0)
+        for t in range(PACK):
+            combine(t, 0)
+        interleave(nc.scalar.copy, hs_bf[0][:], hs[0][:])
+        go_bf = tile("go_bf", [P, P * PACK], BF16, tag="hs0")
+        interleave(nc.scalar.copy, go_bf[:], go_raw[:])
+        combine(0, 1)
+        look_up(2, 1)
+        combine(1, 1)
+        look_up(3, 1)
+        combine(2, 1)
+        nc.vector.reciprocal(rz[:], z[:])
+        combine(3, 1)
+        interleave(nc.scalar.copy, hs_bf[1][:], hs[1][:])
+        nc.vector.tensor_reduce(s[:], by_group(p_rel), AX.X, ALU.add)
+        go_c = tile("go_c", [P, P], U32, tag="link3_1")
+        nc.vector.quantize_mx(out=go_c[:].bitcast(FP8X4), scales=go_s[:], in_=go_bf[:])
+        nc.vector.reciprocal(rs[:], s[:])
+        product(0)
+        nc.vector.tensor_tensor(by_group(wgt[:]), by_group(p_rel), spread(rs[:], GROUPS), ALU.mult)
+        nc.scalar.activation(rest[:], wgt[:], ACT.Identity, bias=sh8[:], scale=-1.0)
+        nc.scalar.activation(k_mean[:], rz[:], ACT.Copy, scale=nsh8[:])
+        nc.scalar.activation(k_out[:], rz[:], ACT.Copy, scale=512.0)
+        nc.scalar.activation(by_group(share[:]), spread(pg, GROUPS), ACT.Copy, scale=k_out[:])
+        product(1)
+        for step in (weigh, group_mean):
+            step(0)
+            step(1)
+        mean_term(0)
+        nc.vector.scalar_tensor_tensor(junk[:], mean[:], k_mean[:], pg, ALU.mult, ALU.mult, accum_out=shift[:])
+        mean_term(1)
+        for step in (add_up, scatter):
+            step(0)
+            step(1)
 
         res = tile("res", [P, T], F32)
         start = 0

@@ -17,13 +17,14 @@ AX = mybir.AxisListType
 
 P = 128
 PACK = 4
-T = 2048
+TOKENS = 2048
 SLOTS = 512
 GROUPS = 64
 GSIZE = 8
 HALF = 256
+LIST_COLS = HALF // 16
+OUT_SCALE = 512.0
 LINEAR_FROM = 30.0
-W_SPLIT = 22
 LAM_FLOOR = 2.0**-60
 STORE_WIDTHS = (256, 512, 512, 512, 256)
 
@@ -45,9 +46,9 @@ def tile_attend_blrlent_bygroup_kernel(
         def spread(ap, groups):
             return ap.unsqueeze(2).to_broadcast([P, groups, GSIZE])
 
-        def load_scales(dst, src, queue):
+        def load_scales(dst, src):
             for quad in range(4):
-                queue.dma_start(
+                nc.sync.dma_start(
                     out=dst[32 * quad : 32 * quad + 4, :].bitcast(I32),
                     in_=src[0, 4 * quad : 4 * quad + 4, :].bitcast(I32),
                 )
@@ -55,40 +56,40 @@ def tile_attend_blrlent_bygroup_kernel(
         def load_words(dst, src):
             nc.sync.dma_start(out=dst[:], in_=src[0].rearrange("p n r -> p (n r)").bitcast(I32))
 
-        def interleave(engine_copy, dst, src):
-            engine_copy(
+        def interleave(dst, src):
+            nc.scalar.copy(
                 out=dst.rearrange("p (c i t) -> p c t i", i=4, t=PACK),
                 in_=src.rearrange("p t (c i) -> p c t i", i=4),
             )
 
-        tab_s = tile("tab_s", [P, T], U8)
-        key_s = tile("key_s", [P, T], U8)
-        gf = tile("gf", [P, T], F32)
+        tab_s = tile("tab_s", [P, TOKENS], U8)
+        key_s = tile("key_s", [P, TOKENS], U8)
+        gf = tile("gf", [P, TOKENS], F32)
         nc.vector.memset(tab_s[:].bitcast(I32), 0)
         nc.gpsimd.memset(key_s[:].bitcast(I32), 0)
         nc.vector.memset(gf[:], 0.0)
 
         idx = tile("idx", [P, SLOTS // 16], U16)
         idx3 = tile("idx3", [P, SLOTS // 16], U16)
-        tab_w = tile("tab_w", [P, T], I32)
-        tab_stage = tile("tab_stage", [P, T], U8)
-        key_w = tile("key_w", [P, T], I32, tag="tab_stage")
+        tab_w = tile("tab_w", [P, TOKENS], I32)
+        tab_stage = tile("tab_stage", [P, TOKENS], U8)
+        key_w = tile("key_w", [P, TOKENS], I32, tag="tab_stage")
         w_raw = [tile("w_raw%d" % h, [P, PACK, HALF], F32) for h in range(2)]
         q_raw = tile("q_raw", [P, PACK, P], F32)
         go_raw = tile("go_raw", [P, PACK, P], F32, tag="w_raw1")
-        old_sb = tile("old_sb", [P, T], F32, tag="key_s")
+        old_sb = tile("old_sb", [P, TOKENS], F32, tag="key_s")
         sharp_sb = tile("sharp_sb", [P, 1], F32, tag="w_raw0")
         lam_sb = tile("lam_sb", [P, PACK], F32, tag="tab_s")
         hsc_sb = tile("hsc_sb", [P, PACK], F32, tag="tab_w")
 
-        load_scales(tab_stage, tab_scales, nc.sync)
+        load_scales(tab_stage, tab_scales)
         nc.sync.dma_start(idx[:], offs)
-        nc.sync.dma_start(out=q_raw[:], in_=query.rearrange("(p j) c -> p j c", j=PACK))
-        load_words(tab_w, tab_words)
         w_rows = w1.rearrange("(p j) c -> p j c", j=PACK)
         for h in range(2):
             nc.sync.dma_start(out=w_raw[h][:], in_=w_rows[:, :, h * HALF : (h + 1) * HALF])
-        load_scales(key_s, keys_scales, nc.sync)
+        load_words(tab_w, tab_words)
+        nc.sync.dma_start(out=q_raw[:], in_=query.rearrange("(p j) c -> p j c", j=PACK))
+        load_scales(key_s, keys_scales)
         nc.sync.dma_start(idx3[:], offs3)
 
         tab_sg = tile("tab_sg", [P, SLOTS], U8)
@@ -102,14 +103,12 @@ def tile_attend_blrlent_bygroup_kernel(
 
         w_bf = tile("w_bf", [P, PACK, P, PACK], BF16)
         q_bf = tile("q_bf", [P, P * PACK], BF16)
-        interleave(nc.scalar.copy, q_bf[:], q_raw[:])
-        for cast, h, lo, hi in (
-            (nc.scalar.copy, 0, 0, 64), (nc.scalar.copy, 1, 0, W_SPLIT), (nc.vector.tensor_copy, 1, W_SPLIT, 64)
-        ):
+        for h, cast in enumerate((nc.scalar.copy, nc.vector.tensor_copy)):
             cast(
-                out=w_bf[:, :, h * 64 + lo : h * 64 + hi, :].rearrange("p t m j -> p m j t"),
-                in_=w_raw[h][:, :, PACK * lo : PACK * hi].rearrange("p j (m t) -> p m j t", t=PACK),
+                out=w_bf[:, :, h * P // 2 : (h + 1) * P // 2, :].rearrange("p t m j -> p m j t"),
+                in_=w_raw[h][:].rearrange("p j (m t) -> p m j t", t=PACK),
             )
+        interleave(q_bf[:], q_raw[:])
         nc.sync.dma_start(out=lam_sb[:], in_=lam.rearrange("(p j) o -> p (j o)", j=PACK))
         nc.sync.dma_start(out=hsc_sb[:], in_=hsc.rearrange("(p j) o -> p (j o)", j=PACK))
         nc.sync.dma_start(out=sharp_sb[:], in_=sharp)
@@ -149,17 +148,15 @@ def tile_attend_blrlent_bygroup_kernel(
         lam_safe = tile("lam_safe", [P, PACK], F32)
         lam_inv = [tile("lam_inv%d" % k, [P, w], F32) for k, w in enumerate((1, 1, 2))]
         nc.vector.tensor_tensor(lam_bump[:], lam_sb[:], lam_sb[:], ALU.mult)
-        a_max_tile = tile("a_max", [P, GROUPS], F32)
-        a_max = a_max_tile[:]
+        a_max = tile("a_max", [P, GROUPS], F32)
         a_sum = tile("a_sum", [P, GROUPS], F32)
-        a_rel_tile = tile("a_rel", [P, SLOTS], F32)
-        a_rel = a_rel_tile[:]
+        a_rel = tile("a_rel", [P, SLOTS], F32)
         nms = tile("nms", [P, GROUPS], F32)
         nms_min = tile("nms_min", [P, 1], F32)
         nc.vector.tensor_scalar(lam_bump[:], lam_bump[:], LAM_FLOOR**2, 2.0 * LAM_FLOOR, ALU.is_lt, ALU.mult)
-        nc.vector.tensor_reduce(a_max, by_group(a_ps[:]), AX.X, ALU.max)
+        nc.vector.tensor_reduce(a_max[:], by_group(a_ps[:]), AX.X, ALU.max)
         nc.vector.tensor_tensor(lam_safe[:], lam_sb[:], lam_bump[:], ALU.add)
-        nc.vector.tensor_tensor(by_group(a_rel), by_group(a_ps[:]), spread(a_max, GROUPS), ALU.subtract)
+        nc.vector.tensor_tensor(by_group(a_rel[:]), by_group(a_ps[:]), spread(a_max[:], GROUPS), ALU.subtract)
         nc.vector.tensor_reduce(a_sum[:], by_group(a_ps[:]), AX.X, ALU.add)
 
         go_s = tile("go_s", [P, P], U8)
@@ -190,11 +187,11 @@ def tile_attend_blrlent_bygroup_kernel(
 
         def look_up(t, h):
             nc.vector.tensor_tensor(
-                link[t][h][:], ht[t][:].indirect(idx3[:, 16 * h : 16 * (h + 1)]),
+                link[t][h][:], ht[t][:].indirect(idx3[:, LIST_COLS * h : LIST_COLS * (h + 1)]),
                 own[t][:, h * HALF : (h + 1) * HALF], ALU.add,
             )
 
-        def combine(t, h):
+        def round_hs(t, h):
             if h == 0:
                 nc.scalar.activation(hs[h][:, t, :], link[t][h][:], ACT.Copy, scale=lh[:, t : t + 1])
             else:
@@ -220,7 +217,7 @@ def tile_attend_blrlent_bygroup_kernel(
         mean = tile("mean", [P, GROUPS], F32)
         term = tile("term", [P, SLOTS], F32)
         inner = tile("inner", [P, SLOTS], F32)
-        junk = tile("junk", [P, GROUPS], F32)
+        shift_parts = tile("shift_parts", [P, GROUPS], F32)
         shift = tile("shift", [P, 1], F32)
 
         def product(h):
@@ -251,7 +248,8 @@ def tile_attend_blrlent_bygroup_kernel(
 
         def scatter(h):
             nc.vector.tensor_tensor(
-                gf[:].indirect(idx[:, 16 * h : 16 * (h + 1)]), inner[:, cols_of(h)], share[:, cols_of(h)], ALU.mult
+                gf[:].indirect(idx[:, LIST_COLS * h : LIST_COLS * (h + 1)]),
+                inner[:, cols_of(h)], share[:, cols_of(h)], ALU.mult,
             )
 
         def add_up(h):
@@ -273,25 +271,26 @@ def tile_attend_blrlent_bygroup_kernel(
         look_up(1, 0)
         softplus(3)
         own_share(3)
-        nc.scalar.activation(p_rel, a_rel, ACT.Exp)
+        nc.scalar.activation(p_rel, a_rel[:], ACT.Exp)
         nc.scalar.activation(pg, nms[:], ACT.Exp, bias=nms_min[:], scale=-1.0, accum_out=z[:])
         look_up(0, 1)
         look_up(1, 1)
         look_up(2, 0)
         look_up(3, 0)
         for t in range(PACK):
-            combine(t, 0)
-        interleave(nc.scalar.copy, hs_bf[0][:], hs[0][:])
+            round_hs(t, 0)
+        interleave(hs_bf[0][:], hs[0][:])
         go_bf = tile("go_bf", [P, P * PACK], BF16, tag="hs0")
-        interleave(nc.scalar.copy, go_bf[:], go_raw[:])
-        combine(0, 1)
+        interleave(go_bf[:], go_raw[:])
+        round_hs(0, 1)
         look_up(2, 1)
-        combine(1, 1)
+        round_hs(1, 1)
         look_up(3, 1)
-        combine(2, 1)
+        round_hs(2, 1)
         nc.vector.reciprocal(rz[:], z[:])
-        combine(3, 1)
-        interleave(nc.scalar.copy, hs_bf[1][:], hs[1][:])
+        round_hs(3, 1)
+        interleave(hs_bf[1][:], hs[1][:])
+
         nc.vector.tensor_reduce(s[:], by_group(p_rel), AX.X, ALU.add)
         go_c = tile("go_c", [P, P], U32, tag="link3_1")
         nc.vector.quantize_mx(out=go_c[:].bitcast(FP8X4), scales=go_s[:], in_=go_bf[:])
@@ -300,20 +299,21 @@ def tile_attend_blrlent_bygroup_kernel(
         nc.vector.tensor_tensor(by_group(wgt[:]), by_group(p_rel), spread(rs[:], GROUPS), ALU.mult)
         nc.scalar.activation(rest[:], wgt[:], ACT.Identity, bias=sh8[:], scale=-1.0)
         nc.scalar.activation(k_mean[:], rz[:], ACT.Copy, scale=nsh8[:])
-        nc.scalar.activation(k_out[:], rz[:], ACT.Copy, scale=512.0)
+        nc.scalar.activation(k_out[:], rz[:], ACT.Copy, scale=OUT_SCALE)
         nc.scalar.activation(by_group(share[:]), spread(pg, GROUPS), ACT.Copy, scale=k_out[:])
         product(1)
+
         for step in (weigh, group_mean):
             step(0)
             step(1)
         mean_term(0)
-        nc.vector.scalar_tensor_tensor(junk[:], mean[:], k_mean[:], pg, ALU.mult, ALU.mult, accum_out=shift[:])
+        nc.vector.scalar_tensor_tensor(shift_parts[:], mean[:], k_mean[:], pg, ALU.mult, ALU.mult, accum_out=shift[:])
         mean_term(1)
         for step in (add_up, scatter):
             step(0)
             step(1)
 
-        res = tile("res", [P, T], F32)
+        res = tile("res", [P, TOKENS], F32)
         start = 0
         for width in STORE_WIDTHS:
             cols = slice(start, start + width)

from contextlib import ExitStack

import concourse.mybir as mybir

FLOPS = 402653184

F32 = mybir.dt.float32
BF16 = mybir.dt.bfloat16
I32 = mybir.dt.int32
U32 = mybir.dt.uint32
U16 = mybir.dt.uint16
U8 = mybir.dt.uint8
FP8X4 = mybir.dt.float8_e4m3fn_x4
ALU = mybir.AluOpType
ACT = mybir.ActivationFunctionType
AX = mybir.AxisListType

P = 128
PACK = 4
TOKENS = 2048
SLOTS = 512
GROUPS = 64
GSIZE = 8
HALF = 256
LIST_COLS = HALF // 16
OUT_SCALE = 512.0
LINEAR_FROM = 30.0
LAM_FLOOR = 2.0**-60
STORE_WIDTHS = (256, 512, 512, 512, 256)


def tile_attend_blrlent_bygroup_kernel(
    tc, query, keys_words, keys_scales, sharp, tab_words, tab_scales, w1, lam, gout, hsc, old, offs3, offs, out
):
    nc = tc.nc
    with ExitStack() as ctx:
        sb = ctx.enter_context(tc.tile_pool(name="sb", bufs=1))
        ps = ctx.enter_context(tc.psum_pool(name="ps", bufs=1))

        def tile(name, shape, dtype, tag=None):
            return sb.tile(shape, dtype, name=name, tag=tag or name, align_bytes=64)

        def by_group(ap):
            return ap.rearrange("p (g j) -> p g j", j=GSIZE)

        def spread(ap, groups):
            return ap.unsqueeze(2).to_broadcast([P, groups, GSIZE])

        def load_scales(dst, src):
            for quad in range(4):
                nc.sync.dma_start(
                    out=dst[32 * quad : 32 * quad + 4, :].bitcast(I32),
                    in_=src[0, 4 * quad : 4 * quad + 4, :].bitcast(I32),
                )

        def load_words(dst, src):
            nc.sync.dma_start(out=dst[:], in_=src[0].rearrange("p n r -> p (n r)").bitcast(I32))

        def interleave(dst, src):
            nc.scalar.copy(
                out=dst.rearrange("p (c i t) -> p c t i", i=4, t=PACK),
                in_=src.rearrange("p t (c i) -> p c t i", i=4),
            )

        tab_s = tile("tab_s", [P, TOKENS], U8)
        key_s = tile("key_s", [P, TOKENS], U8)
        gf = tile("gf", [P, TOKENS], F32)
        nc.vector.memset(tab_s[:].bitcast(I32), 0)
        nc.gpsimd.memset(key_s[:].bitcast(I32), 0)
        nc.vector.memset(gf[:], 0.0)

        idx = tile("idx", [P, SLOTS // 16], U16)
        idx3 = tile("idx3", [P, SLOTS // 16], U16)
        tab_w = tile("tab_w", [P, TOKENS], I32)
        tab_stage = tile("tab_stage", [P, TOKENS], U8)
        key_w = tile("key_w", [P, TOKENS], I32, tag="tab_stage")
        w_raw = [tile("w_raw%d" % h, [P, PACK, HALF], F32) for h in range(2)]
        q_raw = tile("q_raw", [P, PACK, P], F32)
        go_raw = tile("go_raw", [P, PACK, P], F32, tag="w_raw1")
        old_sb = tile("old_sb", [P, TOKENS], F32, tag="key_s")
        sharp_sb = tile("sharp_sb", [P, 1], F32, tag="w_raw0")
        lam_sb = tile("lam_sb", [P, PACK], F32, tag="tab_s")
        hsc_sb = tile("hsc_sb", [P, PACK], F32, tag="tab_w")

        load_scales(tab_stage, tab_scales)
        nc.sync.dma_start(idx[:], offs)
        w_rows = w1.rearrange("(p j) c -> p j c", j=PACK)
        for h in range(2):
            nc.sync.dma_start(out=w_raw[h][:], in_=w_rows[:, :, h * HALF : (h + 1) * HALF])
        load_words(tab_w, tab_words)
        nc.sync.dma_start(out=q_raw[:], in_=query.rearrange("(p j) c -> p j c", j=PACK))
        load_scales(key_s, keys_scales)
        nc.sync.dma_start(idx3[:], offs3)

        tab_sg = tile("tab_sg", [P, SLOTS], U8)
        tab_wg = tile("tab_wg", [P, SLOTS], U32)
        for quad in range(4):
            rows = slice(32 * quad, 32 * quad + 4)
            nc.vector.tensor_copy(tab_s[rows, :].bitcast(I32), tab_stage[rows, :].bitcast(I32))
        load_words(key_w, keys_words)
        nc.vector.tensor_copy(tab_sg[:], tab_s[:].indirect(idx[:]))
        nc.vector.tensor_copy(tab_wg[:], tab_w[:].bitcast(U32).indirect(idx[:]))

        w_bf = tile("w_bf", [P, PACK, P, PACK], BF16)
        q_bf = tile("q_bf", [P, P * PACK], BF16)
        for h, cast in enumerate((nc.scalar.copy, nc.vector.tensor_copy)):
            cast(
                out=w_bf[:, :, h * P // 2 : (h + 1) * P // 2, :].rearrange("p t m j -> p m j t"),
                in_=w_raw[h][:].rearrange("p j (m t) -> p m j t", t=PACK),
            )
        interleave(q_bf[:], q_raw[:])
        nc.sync.dma_start(out=lam_sb[:], in_=lam.rearrange("(p j) o -> p (j o)", j=PACK))
        nc.sync.dma_start(out=hsc_sb[:], in_=hsc.rearrange("(p j) o -> p (j o)", j=PACK))
        nc.sync.dma_start(out=sharp_sb[:], in_=sharp)
        nc.sync.dma_start(out=go_raw[:], in_=gout.rearrange("(p j) c -> p j c", j=PACK))
        w_c = tile("w_c", [P, PACK * P], U32)
        w_s = tile("w_s", [P, PACK * P], U8)
        zh = [ps.tile([P, SLOTS], F32, name="zh%d" % t) for t in range(PACK)]
        ex = [tile("ex%d" % t, [P, SLOTS], F32) for t in range(PACK)]
        for t in range(PACK):
            cols = slice(t * P, (t + 1) * P)
            nc.vector.quantize_mx(
                out=w_c[:, cols].bitcast(FP8X4), scales=w_s[:, cols], in_=w_bf[:, t].rearrange("p m j -> p (m j)")
            )
            nc.tensor.matmul_mx(
                out=zh[t][:], lhsT=w_c[:, cols].bitcast(FP8X4), lhsT_scale=w_s[:, cols],
                rhs=tab_wg[:].bitcast(FP8X4), rhs_scale=tab_sg[:], start=True, stop=True,
            )
            nc.scalar.activation(ex[t][:], zh[t][:], ACT.Exp)

        key_wg = tile("key_wg", [P, SLOTS], U32)
        key_sg = tile("key_sg", [P, SLOTS], U8, tag="w_bf")
        nc.vector.tensor_copy(key_sg[:], key_s[:].indirect(idx[:]))
        nc.sync.dma_start(out=old_sb[:], in_=old)
        q_c = tile("q_c", [P, P], U32)
        q_s = tile("q_s", [P, P], U8)
        nc.vector.quantize_mx(out=q_c[:].bitcast(FP8X4), scales=q_s[:], in_=q_bf[:])
        nc.vector.tensor_copy(key_wg[:], key_w[:].bitcast(U32).indirect(idx[:]))
        a_ps = ps.tile([P, SLOTS], F32, name="a_ps")
        nc.tensor.matmul_mx(
            out=a_ps[:], lhsT=q_c[:].bitcast(FP8X4), lhsT_scale=q_s[:],
            rhs=key_wg[:].bitcast(FP8X4), rhs_scale=key_sg[:], start=True, stop=True,
        )
        sh8 = tile("sh8", [P, 1], F32)
        nsh8 = tile("nsh8", [P, 1], F32)
        lh = tile("lh", [P, PACK], F32)
        lam_bump = tile("lam_bump", [P, PACK], F32)
        lam_safe = tile("lam_safe", [P, PACK], F32)
        lam_inv = [tile("lam_inv%d" % k, [P, w], F32) for k, w in enumerate((1, 1, 2))]
        nc.vector.tensor_tensor(lam_bump[:], lam_sb[:], lam_sb[:], ALU.mult)
        a_max = tile("a_max", [P, GROUPS], F32)
        a_sum = tile("a_sum", [P, GROUPS], F32)
        a_rel = tile("a_rel", [P, SLOTS], F32)
        nms = tile("nms", [P, GROUPS], F32)
        nms_min = tile("nms_min", [P, 1], F32)
        nc.vector.tensor_scalar(lam_bump[:], lam_bump[:], LAM_FLOOR**2, 2.0 * LAM_FLOOR, ALU.is_lt, ALU.mult)
        nc.vector.tensor_reduce(a_max[:], by_group(a_ps[:]), AX.X, ALU.max)
        nc.vector.tensor_tensor(lam_safe[:], lam_sb[:], lam_bump[:], ALU.add)
        nc.vector.tensor_tensor(by_group(a_rel[:]), by_group(a_ps[:]), spread(a_max[:], GROUPS), ALU.subtract)
        nc.vector.tensor_reduce(a_sum[:], by_group(a_ps[:]), AX.X, ALU.add)

        go_s = tile("go_s", [P, P], U8)

        ln_tags = ("ln0", "ln1", "lam_inv0", "lam_inv1")
        ln = [tile("ln%d" % t, [P, SLOTS], F32, tag=ln_tags[t]) for t in range(PACK)]
        ht = [tile("ht%d" % t, [P, SLOTS], F32, tag=(("a_max",) + ln_tags)[t]) for t in range(PACK)]
        own = [tile("own%d" % t, [P, SLOTS], F32) for t in range(PACK)]
        link = [[tile("link%d_%d" % (t, h), [P, HALF], F32) for h in range(2)] for t in range(PACK)]
        hs = [tile("hs%d" % h, [P, PACK, HALF], BF16) for h in range(2)]
        nc.vector.reciprocal(lam_inv[0][:], lam_safe[:, 0:1])
        nc.vector.reciprocal(lam_inv[1][:], lam_safe[:, 1:2])
        nc.vector.reciprocal(lam_inv[2][:], lam_safe[:, 2:4])
        nc.vector.tensor_tensor(lh[:], lam_safe[:], hsc_sb[:], ALU.mult)
        nc.vector.tensor_scalar(sh8[:], sharp_sb[:], 1.0 / GSIZE, None, ALU.mult)
        nc.vector.tensor_scalar(nsh8[:], sharp_sb[:], -1.0 / GSIZE, None, ALU.mult)
        nc.vector.tensor_scalar(nms[:], a_sum[:], nsh8[:], None, ALU.mult, ALU.min, accum_out=nms_min[:])
        inv_cols = (lam_inv[0][:], lam_inv[1][:], lam_inv[2][:, 0:1], lam_inv[2][:, 1:2])

        def log1p(t):
            nc.scalar.activation(ln[t][:], ex[t][:], ACT.Ln, bias=1.0)

        def softplus(t):
            nc.vector.scalar_tensor_tensor(ht[t][:], ln[t][:], LINEAR_FROM, zh[t][:], ALU.min, ALU.max)

        def own_share(t):
            nc.scalar.activation(own[t][:], ht[t][:], ACT.Copy, scale=inv_cols[t])

        def look_up(t, h):
            nc.vector.tensor_tensor(
                link[t][h][:], ht[t][:].indirect(idx3[:, LIST_COLS * h : LIST_COLS * (h + 1)]),
                own[t][:, h * HALF : (h + 1) * HALF], ALU.add,
            )

        def round_hs(t, h):
            if h == 0:
                nc.scalar.activation(hs[h][:, t, :], link[t][h][:], ACT.Copy, scale=lh[:, t : t + 1])
            else:
                nc.vector.tensor_scalar(hs[h][:, t, :], link[t][h][:], lh[:, t : t + 1], None, ALU.mult)

        late_exp = tile("late_exp", [P, SLOTS + GROUPS], F32, tag="ex%d" % (PACK - 1))
        p_rel = late_exp[:, :SLOTS]
        pg = late_exp[:, SLOTS:]
        s = tile("s", [P, GROUPS], F32, tag="link2_1")
        z = tile("z", [P, 1], F32)

        hs_bf = [tile("hs_bf%d" % h, [P, HALF * PACK], BF16) for h in range(2)]
        hs_s = [tile("hs_s%d" % h, [P, HALF], U8) for h in range(2)]
        c0 = [ps.tile([P, HALF], F32, name="c0_%d" % h) for h in range(2)]
        rs = tile("rs", [P, GROUPS], F32)
        rz = tile("rz", [P, 1], F32)
        wgt = tile("wgt", [P, SLOTS], F32)
        rest = tile("rest", [P, SLOTS], F32)
        k_out = tile("k_out", [P, 1], F32)
        k_mean = tile("k_mean", [P, 1], F32)
        share = tile("share", [P, SLOTS], F32)
        cw = tile("cw", [P, SLOTS], F32)
        mean = tile("mean", [P, GROUPS], F32)
        term = tile("term", [P, SLOTS], F32)
        inner = tile("inner", [P, SLOTS], F32)
        shift_parts = tile("shift_parts", [P, GROUPS], F32)
        shift = tile("shift", [P, 1], F32)

        def product(h):
            codes = tile("hs_c%d" % h, [P, HALF], U32, tag=("link2_1", "rs")[h])
            nc.vector.quantize_mx(out=codes[:].bitcast(FP8X4), scales=hs_s[h][:], in_=hs_bf[h][:])
            nc.tensor.matmul_mx(
                out=c0[h][:], lhsT=go_c[:].bitcast(FP8X4), lhsT_scale=go_s[:],
                rhs=codes[:].bitcast(FP8X4), rhs_scale=hs_s[h][:], start=True, stop=True,
            )

        def cols_of(h):
            return slice(h * HALF, (h + 1) * HALF)

        def groups_of(h):
            return slice(h * GROUPS // 2, (h + 1) * GROUPS // 2)

        def weigh(h):
            nc.vector.tensor_tensor(cw[:, cols_of(h)], c0[h][:], wgt[:, cols_of(h)], ALU.mult)

        def group_mean(h):
            nc.vector.tensor_reduce(mean[:, groups_of(h)], by_group(cw[:, cols_of(h)]), AX.X, ALU.add)

        def mean_term(h):
            nc.vector.tensor_tensor(
                by_group(term[:, cols_of(h)]), by_group(rest[:, cols_of(h)]),
                spread(mean[:, groups_of(h)], GROUPS // 2), ALU.mult,
            )

        def scatter(h):
            nc.vector.tensor_tensor(
                gf[:].indirect(idx[:, LIST_COLS * h : LIST_COLS * (h + 1)]),
                inner[:, cols_of(h)], share[:, cols_of(h)], ALU.mult,
            )

        def add_up(h):
            nc.vector.scalar_tensor_tensor(
                inner[:, cols_of(h)], term[:, cols_of(h)], shift[:], cw[:, cols_of(h)], ALU.add, ALU.add
            )

        log1p(0)
        log1p(1)
        softplus(0)
        own_share(0)
        log1p(2)
        softplus(1)
        own_share(1)
        log1p(3)
        look_up(0, 0)
        softplus(2)
        own_share(2)
        look_up(1, 0)
        softplus(3)
        own_share(3)
        nc.scalar.activation(p_rel, a_rel[:], ACT.Exp)
        nc.scalar.activation(pg, nms[:], ACT.Exp, bias=nms_min[:], scale=-1.0, accum_out=z[:])
        look_up(0, 1)
        look_up(1, 1)
        look_up(2, 0)
        look_up(3, 0)
        for t in range(PACK):
            round_hs(t, 0)
        interleave(hs_bf[0][:], hs[0][:])
        go_bf = tile("go_bf", [P, P * PACK], BF16, tag="hs0")
        interleave(go_bf[:], go_raw[:])
        round_hs(0, 1)
        look_up(2, 1)
        round_hs(1, 1)
        look_up(3, 1)
        round_hs(2, 1)
        nc.vector.reciprocal(rz[:], z[:])
        round_hs(3, 1)
        interleave(hs_bf[1][:], hs[1][:])

        nc.vector.tensor_reduce(s[:], by_group(p_rel), AX.X, ALU.add)
        go_c = tile("go_c", [P, P], U32, tag="link3_1")
        nc.vector.quantize_mx(out=go_c[:].bitcast(FP8X4), scales=go_s[:], in_=go_bf[:])
        nc.vector.reciprocal(rs[:], s[:])
        product(0)
        nc.vector.tensor_tensor(by_group(wgt[:]), by_group(p_rel), spread(rs[:], GROUPS), ALU.mult)
        nc.scalar.activation(rest[:], wgt[:], ACT.Identity, bias=sh8[:], scale=-1.0)
        nc.scalar.activation(k_mean[:], rz[:], ACT.Copy, scale=nsh8[:])
        nc.scalar.activation(k_out[:], rz[:], ACT.Copy, scale=OUT_SCALE)
        nc.scalar.activation(by_group(share[:]), spread(pg, GROUPS), ACT.Copy, scale=k_out[:])
        product(1)

        for step in (weigh, group_mean):
            step(0)
            step(1)
        mean_term(0)
        nc.vector.scalar_tensor_tensor(shift_parts[:], mean[:], k_mean[:], pg, ALU.mult, ALU.mult, accum_out=shift[:])
        mean_term(1)
        for step in (add_up, scatter):
            step(0)
            step(1)

        res = tile("res", [P, TOKENS], F32)
        start = 0
        for width in STORE_WIDTHS:
            cols = slice(start, start + width)
            nc.vector.tensor_tensor(res[:, cols], gf[:, cols], old_sb[:, cols], ALU.add)
            nc.sync.dma_start(out=out[:, cols], in_=res[:, cols])
            start += width
